import numpy as np
import ml_dtypes


def mxq(x, axis, fmt="e4m3"):
    dtype, down = {"e4m3": (ml_dtypes.float8_e4m3fn, 7), "e5m2": (ml_dtypes.float8_e5m2, 14)}[fmt]
    v = np.moveaxis(np.asarray(x, np.float32).astype(ml_dtypes.bfloat16).astype(np.float64), axis, -1)
    blocks = v.reshape(v.shape[:-1] + (-1, 32))
    amax = np.abs(blocks).max(-1, keepdims=True)
    byte = np.maximum(np.where(amax > 0, np.frexp(amax)[1] - 1 + 127, 0) - down, 1)
    scale = np.exp2(byte - 127.0)
    codes = (blocks / scale).astype(np.float32).astype(dtype).astype(np.float64)
    return np.moveaxis((codes * scale).reshape(v.shape), -1, axis)


WIDE = False


def mx_kscale(k):
    if not WIDE:
        return np.ones(k)
    levels = np.array([10, -10, 5, -5, 0])
    if k % 512:
        return np.exp2(np.random.permutation(np.resize(levels, k // 32))).repeat(32)
    a = np.empty((k // 512, 16))
    for p in range(k // 512):
        a[p, :8] = np.random.permutation(np.resize(levels, 8))
        for g in range(8):
            far = levels[np.abs(levels - a[p, g]) >= 10]
            a[p, g + 8] = far[np.random.randint(len(far))]
    return np.exp2(a.ravel()).repeat(32)


def f64(x):
    return np.asarray(x).astype(np.float64)


def striped(idx):
    return np.tile(idx.reshape(-1, 16).T, (8, 1)).astype(np.uint16)


def unstriped(offs):
    return offs[:16].T.reshape(-1).astype(np.int64)


E2M1 = np.array([0.0, 0.5, 1.0, 1.5, 2.0, 3.0, 4.0, 6.0, -0.0, -0.5, -1.0, -1.5, -2.0, -3.0, -4.0, -6.0])


def pack_weight(w, fmt):
    k, n = w.shape
    w = f64(np.asarray(w, np.float32).astype(ml_dtypes.bfloat16)).reshape(k // 32, 32, n)
    amax = np.abs(w).max(1)
    if fmt == "e4m3":
        byte = np.frexp(amax)[1] - 1 + 127 - 7
    else:
        mant, ex = np.frexp(amax / 6.0)
        byte = np.where(mant > 0.5, ex, ex - 1) + 127
    byte = np.clip(np.where(amax > 0, byte, 1), 1, 254)
    scaled = (w * np.exp2(127.0 - byte)[:, None, :]).reshape(k, n).astype(np.float32)
    by_word = np.ascontiguousarray(scaled.reshape(k // 512, 128, 4, n).transpose(0, 1, 3, 2))
    if fmt == "e4m3":
        words = by_word.astype(ml_dtypes.float8_e4m3fn).view(np.uint8)
    else:
        c = by_word.astype(ml_dtypes.float4_e2m1fn).view(np.uint8) & 0xF
        words = (c[..., 0::2] | (c[..., 1::2] << 4)).reshape(k // 512, 128, 2 * n)
    return np.ascontiguousarray(words), np.ascontiguousarray(byte.astype(np.uint8).reshape(k // 512, 16, n))


def unpack_weight(words, scales, fmt):
    g, _, n = scales.shape
    words = np.ascontiguousarray(words).reshape(g, 128, n, -1)
    if fmt == "e4m3":
        vals = words.view(ml_dtypes.float8_e4m3fn).astype(np.float64)
    else:
        nib = np.empty((g, 128, n, 4), np.uint8)
        nib[..., 0::2] = words & 0xF
        nib[..., 1::2] = words >> 4
        vals = E2M1[nib]
    vals = vals * np.repeat(np.exp2(scales.astype(np.float64) - 127.0), 8, axis=1)[..., None]
    return vals.transpose(0, 1, 3, 2).reshape(g * 512, n)


def relu2(v):
    return np.maximum(v, 0.0) ** 2


K, T, E, N = 1536, 512, 4, 512
COUNTS = (128, 256, 256, 384)
STARTS = np.cumsum((0,) + COUNTS)


def by_expert(wq, xq):
    return np.concatenate([wq[e].T @ xq[:, STARTS[e]:STARTS[e + 1]] for e in range(E)], axis=1)


def setup_inputs():
    n = np.random.standard_normal
    s = mx_kscale(K)[:, None]
    both = np.repeat(np.arange(E), COUNTS)
    pair = np.stack([both[:T], both[T:]])[:, np.random.permutation(T)]
    pair = np.where(np.random.rand(T) < 0.5, pair, pair[::-1])
    for _ in range(8):
        s_, t_ = np.random.permutation(T).reshape(2, -1); r = np.random.randint(2, size=T // 2); q = np.random.randint(2, size=T // 2); x, y = pair[r, s_].copy(), pair[q, t_].copy()
        ok = (pair[1 - r, s_] != y) & (pair[1 - q, t_] != x); pair[r[ok], s_[ok]] = y[ok]; pair[q[ok], t_[ok]] = x[ok]
    order = np.argsort(pair.reshape(-1), kind="stable")
    slot_token = order % T; pos = np.empty(2 * T, np.int64); pos[order] = np.arange(2 * T); pos = pos.reshape(2, T)
    g = np.random.uniform(0.2, 0.8, T)
    w = [pack_weight(m, "e2m1") for m in n((E, K, N)) / np.sqrt(K) / s[None]]
    return {
        "xT": (n((K, T)) * s).astype(np.float32),
        "w_words": np.stack([m[0] for m in w]),
        "w_scales": np.stack([m[1] for m in w]),
        "b": (0.3 * n((N, E))).astype(np.float32),
        "gate": np.stack([np.tile(g, (N, 1)), np.tile(1.0 - g, (N, 1))]).astype(np.float32),
        "offs": striped(slot_token),
        "pos1": striped(pos[0]),
        "pos2": striped(pos[1]),
    }


def reference(xT, w_words, w_scales, b, gate, offs, pos1, pos2):
    idx = unstriped(offs)
    w = np.stack([unpack_weight(w_words[e], w_scales[e], "e2m1") for e in range(E)])
    xq = mxq(f64(xT)[:, idx], 0, "e4m3")
    y = by_expert(w, xq)
    y = relu2(y + np.repeat(f64(b), COUNTS, axis=1))
    return f64(gate[0]) * y[:, unstriped(pos1)] + f64(gate[1]) * y[:, unstriped(pos2)]

@@ -1,0 +1,167 @@
+from contextlib import ExitStack
+
+import concourse.mybir as mybir
+
+K, T, E, N = 1536, 512, 4, 512
+COUNTS = (128, 256, 256, 384)
+STARTS = (0, 128, 384, 640)
+SLOTS = 1024
+P = 128
+PASSES = K // 512
+NT = N // P
+
+F32 = mybir.dt.float32
+BF16 = mybir.dt.bfloat16
+U32 = mybir.dt.uint32
+I32 = mybir.dt.int32
+U16 = mybir.dt.uint16
+U8 = mybir.dt.uint8
+FP8X4 = mybir.dt.float8_e4m3fn_x4
+FP4X4 = mybir.dt.float4_e2m1fn_x4
+ACT = mybir.ActivationFunctionType
+MULT = mybir.AluOpType.mult
+ADD = mybir.AluOpType.add
+
+FLOPS = 2 * K * N * SLOTS
+
+PIECES = ((640, 1024), (256, 640), (0, 256))
+LAST_PIECES = ((640, 1024), (256, 640), (128, 256), (0, 128))
+
+
+def expert_of(slot):
+    return max(e for e in range(E) if STARTS[e] <= slot)
+
+
+def tile_moe_rag_lin_relu2_kernel(tc, xT, w_words, w_scales, b, gate, offs, pos1, pos2, out):
+    nc = tc.nc
+    with ExitStack() as ctx:
+        keep = ctx.enter_context(tc.tile_pool(name="keep", bufs=1))
+        psum = ctx.enter_context(tc.psum_pool(name="psum", bufs=1))
+
+        offs_t = keep.tile([P, SLOTS // 16], U16, name="offs_t")
+        pos1_t = keep.tile([P, T // 16], U16, name="pos1_t")
+        pos2_t = keep.tile([P, T // 16], U16, name="pos2_t")
+        raw = [keep.tile([P, 4, T], F32, name=f"raw{a}") for a in range(PASSES)]
+        grouped = [keep.tile([P, T, 4], BF16, name=f"grouped{a}", align_bytes=64) for a in range(PASSES)]
+        codes = [keep.tile([P, T], U32, name=f"codes{a}", align_bytes=64) for a in range(PASSES)]
+        scales01 = keep.tile([P, T], U8, name="scales01", align_bytes=64)
+        scales2 = keep.tile([P, T], U8, name="scales2", align_bytes=64)
+        slot_words = [keep.tile([P, SLOTS], U32, name=f"slot_words{a}", align_bytes=64) for a in range(PASSES)]
+        slot_bytes01 = keep.tile([P, SLOTS], U8, name="slot_bytes01", align_bytes=64)
+        slot_bytes0 = keep.tile([P, SLOTS], U8, name="slot_bytes0", align_bytes=64)
+        slot_bytes2 = keep.tile([P, SLOTS], U8, name="slot_bytes2", align_bytes=64)
+        slot_bytes = [slot_bytes0, slot_bytes01, slot_bytes2]
+        w_t = [keep.tile([P, PASSES, 2 * N], U8, name=f"w{e}", align_bytes=64) for e in range(E)]
+        ws_t = keep.tile([P, E * PASSES, N], U8, name="ws_t", align_bytes=64)
+        b_t = keep.tile([P, NT, E], F32, name="b_t")
+        gate_t = [keep.tile([P, 2, T], F32, name=f"gate{t}") for t in range(NT)]
+        r_t = [keep.tile([P, SLOTS], F32, name=f"r{t}") for t in range(NT)]
+        y_t = [keep.tile([P, SLOTS], F32, name=f"y{t}") for t in range(NT)]
+        one_t = [keep.tile([P, T], F32, name=f"one{t}") for t in range(NT)]
+        two_t = [keep.tile([P, T], F32, name=f"two{t}") for t in range(NT)]
+        sum_t = [keep.tile([P, T], F32, name=f"sum{t}") for t in range(NT)]
+        warm = keep.tile([P, 1], F32, name="warm")
+        bank_a = [psum.tile([P, 512], F32, name=f"bank_a{t}") for t in range(NT)]
+        bank_b = [psum.tile([P, 512], F32, name=f"bank_b{t}") for t in range(NT)]
+
+        def bank(t, lo, hi):
+            if hi <= 128:
+                return bank_a[t][:, lo:hi]
+            if lo >= 640:
+                return bank_a[t][:, lo - 512 : hi - 512]
+            return bank_b[t][:, lo - 128 : hi - 128]
+
+        def load_x(a, lo, hi):
+            nc.sync.dma_start(out=raw[a][:, :, lo:hi], in_=xT[512 * a : 512 * (a + 1), lo:hi].rearrange("(p j) w -> p j w", j=4))
+
+        load_x(0, 0, 256)
+        load_x(0, 256, T)
+        nc.sync.dma_start(offs_t[:], offs)
+        load_x(1, 0, T)
+        load_x(2, 0, T)
+        nc.vector.memset(ws_t[:].rearrange("p a n -> p (a n)").bitcast(I32), 0)
+        nc.gpsimd.memset(scales01[:], 0)
+        nc.gpsimd.memset(scales2[:], 0)
+        nc.gpsimd.memset(slot_bytes0[:], 0)
+        nc.vector.memset(warm[:], 0.0)
+        nc.scalar.activation(warm[:], warm[:], ACT.Relu)
+        by_row = w_scales.rearrange("e a q n -> q (e a) n")
+        for q in range(4):
+            nc.sync.dma_start(out=ws_t[32 * q : 32 * q + 4, :, :].bitcast(I32), in_=by_row[4 * q : 4 * q + 4, :, :].bitcast(I32))
+        for e in (3, 2, 1, 0):
+            nc.sync.dma_start(out=w_t[e][:], in_=w_words[e].rearrange("a p n -> p a n"))
+        nc.sync.dma_start(out=b_t[:], in_=b.rearrange("(t p) e -> p t e", p=P))
+        nc.sync.dma_start(pos1_t[:], pos1)
+        nc.sync.dma_start(pos2_t[:], pos2)
+        for t in range(NT):
+            nc.sync.dma_start(out=gate_t[t][:], in_=gate[:, P * t : P * (t + 1), :].rearrange("c p w -> p c w"))
+
+        def cast(engine_copy, a, lo, hi):
+            engine_copy(out=grouped[a][:, lo:hi, :], in_=raw[a][:, :, lo:hi].rearrange("p j w -> p w j"))
+
+        def quantize(a, plane, lo, hi):
+            nc.vector.quantize_mx(
+                out=codes[a][:, lo:hi].bitcast(FP8X4), scales=plane[:, lo:hi], in_=grouped[a][:, lo:hi, :].rearrange("p w j -> p (w j)")
+            )
+
+        def gather(out, table, pieces):
+            for lo, hi in pieces:
+                nc.vector.tensor_copy(out[:, lo:hi], table[:].indirect(offs_t[:, lo // 16 : hi // 16]))
+
+        cast(nc.vector.tensor_copy, 0, 0, 256)
+        quantize(0, scales01[4:P, :], 0, 256)
+        cast(nc.vector.tensor_copy, 0, 256, 416)
+        cast(nc.scalar.copy, 0, 416, T)
+        quantize(0, scales01[4:P, :], 256, T)
+        for a in range(1, PASSES):
+            cast(nc.scalar.copy, a, 0, T // 2)
+            cast(nc.scalar.copy, a, T // 2, T)
+        gather(slot_words[0], codes[0], PIECES)
+        quantize(1, scales01, 0, T)
+        gather(slot_bytes01, scales01, PIECES)
+        for q in range(4):
+            nc.scalar.dma_start(
+                out=slot_bytes0[32 * q : 32 * q + 4, :].bitcast(I32), in_=slot_bytes01[32 * q + 4 : 32 * q + 8, :].bitcast(I32)
+            )
+        gather(slot_words[1], codes[1], PIECES)
+        quantize(2, scales2, 0, T)
+        for lo, hi in LAST_PIECES:
+            if lo == 128:
+                gather(slot_bytes2, scales2, ((0, 256),))
+            elif lo > 128:
+                gather(slot_bytes2, scales2, ((lo, hi),))
+            gather(slot_words[2], codes[2], ((lo, hi),))
+
+        def multiply(t, s, passes):
+            e = expert_of(s)
+            for a in passes:
+                nc.tensor.matmul_mx(
+                    out=bank(t, s, s + P),
+                    lhsT=w_t[e][:, a, 2 * P * t : 2 * P * (t + 1)].bitcast(FP4X4),
+                    lhsT_scale=ws_t[:, PASSES * e + a, P * t : P * (t + 1)],
+                    rhs=slot_words[a][:, s : s + P].bitcast(FP8X4),
+                    rhs_scale=slot_bytes[a][:, s : s + P],
+                    start=(a == 0),
+                    stop=(a == PASSES - 1),
+                )
+
+        def relu2(t, e):
+            lo, hi = STARTS[e], STARTS[e] + COUNTS[e]
+            nc.scalar.activation(r_t[t][:, lo:hi], bank(t, lo, hi), ACT.Relu, bias=b_t[:, t, e : e + 1])
+            nc.scalar.activation(y_t[t][:, lo:hi], r_t[t][:, lo:hi], ACT.Square)
+
+        early = (640, 512)
+        for t in range(NT):
+            for s in early:
+                multiply(t, s, (0, 1))
+
+        for t in range(NT):
+            for e, chunks in ((3, (640, 768, 896)), (2, (512, 384)), (1, (256, 128)), (0, (0,))):
+                for s in chunks:
+                    multiply(t, s, (2,) if s in early else (0, 1, 2))
+                relu2(t, e)
+            nc.vector.tensor_tensor(one_t[t][:], y_t[t][:].indirect(pos1_t[:]), gate_t[t][:, 0, :], MULT)
+            nc.vector.tensor_tensor(two_t[t][:], y_t[t][:].indirect(pos2_t[:]), gate_t[t][:, 1, :], MULT)
+            for lo, hi in ((0, T),) if t < NT - 1 else ((0, T // 2), (T // 2, T)):
+                nc.vector.tensor_tensor(sum_t[t][:, lo:hi], one_t[t][:, lo:hi], two_t[t][:, lo:hi], ADD)
+                nc.sync.dma_start(out=out[P * t : P * (t + 1), lo:hi], in_=sum_t[t][:, lo:hi])

@@ -116,15 +116,17 @@ def tile_moe_rag_lin_relu2_kernel(tc, xT, w_words, w_scales, b, gate, offs, pos1
         for a in range(1, PASSES):
             cast(nc.scalar.copy, a, 0, T // 2)
             cast(nc.scalar.copy, a, T // 2, T)
-        gather(slot_words[0], codes[0], PIECES)
+        gather(slot_words[0], codes[0], PIECES[:2])
         quantize(1, scales01, 0, T)
+        gather(slot_words[0], codes[0], PIECES[2:])
         gather(slot_bytes01, scales01, PIECES)
         for q in range(4):
             nc.scalar.dma_start(
                 out=slot_bytes0[32 * q : 32 * q + 4, :].bitcast(I32), in_=slot_bytes01[32 * q + 4 : 32 * q + 8, :].bitcast(I32)
             )
-        gather(slot_words[1], codes[1], PIECES)
+        gather(slot_words[1], codes[1], PIECES[:2])
         quantize(2, scales2, 0, T)
+        gather(slot_words[1], codes[1], PIECES[2:])
         for lo, hi in LAST_PIECES:
             if lo == 128:
                 gather(slot_bytes2, scales2, ((0, 256),))
@@ -145,9 +147,12 @@ def tile_moe_rag_lin_relu2_kernel(tc, xT, w_words, w_scales, b, gate, offs, pos1
                     stop=(a == PASSES - 1),
                 )
 
-        def relu2(t, e):
+        def relu(t, e):
             lo, hi = STARTS[e], STARTS[e] + COUNTS[e]
             nc.scalar.activation(r_t[t][:, lo:hi], bank(t, lo, hi), ACT.Relu, bias=b_t[:, t, e : e + 1])
+
+        def square(t, e):
+            lo, hi = STARTS[e], STARTS[e] + COUNTS[e]
             nc.scalar.activation(y_t[t][:, lo:hi], r_t[t][:, lo:hi], ACT.Square)
 
         early = (640, 512)
@@ -155,13 +160,23 @@ def tile_moe_rag_lin_relu2_kernel(tc, xT, w_words, w_scales, b, gate, offs, pos1
             for s in early:
                 multiply(t, s, (0, 1))
 
+        halves = ((0, T // 2), (T // 2, T))
         for t in range(NT):
+            before = None
             for e, chunks in ((3, (640, 768, 896)), (2, (512, 384)), (1, (256, 128)), (0, (0,))):
                 for s in chunks:
                     multiply(t, s, (2,) if s in early else (0, 1, 2))
-                relu2(t, e)
+                relu(t, e)
+                if before is not None:
+                    square(t, before)
+                before = e
+            square(t, before)
             nc.vector.tensor_tensor(one_t[t][:], y_t[t][:].indirect(pos1_t[:]), gate_t[t][:, 0, :], MULT)
-            nc.vector.tensor_tensor(two_t[t][:], y_t[t][:].indirect(pos2_t[:]), gate_t[t][:, 1, :], MULT)
-            for lo, hi in ((0, T),) if t < NT - 1 else ((0, T // 2), (T // 2, T)):
+            for lo, hi in halves:
+                nc.vector.tensor_tensor(two_t[t][:, lo:hi], y_t[t][:].indirect(pos2_t[:, lo // 16 : hi // 16]), gate_t[t][:, 1, lo:hi], MULT)
+            for lo, hi in halves:
                 nc.vector.tensor_tensor(sum_t[t][:, lo:hi], one_t[t][:, lo:hi], two_t[t][:, lo:hi], ADD)
-                nc.sync.dma_start(out=out[P * t : P * (t + 1), lo:hi], in_=sum_t[t][:, lo:hi])
+                if t == NT - 1:
+                    (nc.sync if lo == 0 else nc.scalar).dma_start(out=out[P * t : P * (t + 1), lo:hi], in_=sum_t[t][:, lo:hi])
+            if t < NT - 1:
+                nc.sync.dma_start(out=out[P * t : P * (t + 1), :], in_=sum_t[t][:])

@@ -25,7 +25,6 @@ ADD = mybir.AluOpType.add
 FLOPS = 2 * K * N * SLOTS
 
 PIECES = ((640, 1024), (256, 640), (0, 256))
-LAST_PIECES = ((640, 1024), (256, 640), (128, 256), (0, 128))
 
 
 def expert_of(slot):
@@ -97,7 +96,10 @@ def tile_moe_rag_lin_relu2_kernel(tc, xT, w_words, w_scales, b, gate, offs, pos1
             nc.sync.dma_start(out=gate_t[t][:], in_=gate[:, P * t : P * (t + 1), :].rearrange("c p w -> p c w"))
 
         def cast(engine_copy, a, lo, hi):
-            engine_copy(out=grouped[a][:, lo:hi, :], in_=raw[a][:, :, lo:hi].rearrange("p j w -> p w j"))
+            engine_copy(
+                out=grouped[a][:, lo:hi, :].rearrange("p (c i) j -> p c j i", i=4),
+                in_=raw[a][:, :, lo:hi].rearrange("p j (c i) -> p c j i", i=4),
+            )
 
         def quantize(a, plane, lo, hi):
             nc.vector.quantize_mx(
@@ -113,26 +115,27 @@ def tile_moe_rag_lin_relu2_kernel(tc, xT, w_words, w_scales, b, gate, offs, pos1
         cast(nc.vector.tensor_copy, 0, 256, 416)
         cast(nc.scalar.copy, 0, 416, T)
         quantize(0, scales01[4:P, :], 256, T)
-        for a in range(1, PASSES):
-            cast(nc.scalar.copy, a, 0, T // 2)
-            cast(nc.scalar.copy, a, T // 2, T)
-        gather(slot_words[0], codes[0], PIECES[:2])
+        cast(nc.scalar.copy, 1, 192, T)
+        cast(nc.scalar.copy, 2, 0, T // 2)
+        cast(nc.scalar.copy, 2, T // 2, T)
+        first, second, third = PIECES
+        gather(slot_words[0], codes[0], (first, second))
+        cast(nc.vector.tensor_copy, 1, 0, 192)
+        gather(slot_words[0], codes[0], (third,))
         quantize(1, scales01, 0, T)
-        gather(slot_words[0], codes[0], PIECES[2:])
         gather(slot_bytes01, scales01, PIECES)
         for q in range(4):
             nc.scalar.dma_start(
                 out=slot_bytes0[32 * q : 32 * q + 4, :].bitcast(I32), in_=slot_bytes01[32 * q + 4 : 32 * q + 8, :].bitcast(I32)
             )
-        gather(slot_words[1], codes[1], PIECES[:2])
+        gather(slot_words[1], codes[1], (first, second))
         quantize(2, scales2, 0, T)
-        gather(slot_words[1], codes[1], PIECES[2:])
-        for lo, hi in LAST_PIECES:
-            if lo == 128:
-                gather(slot_bytes2, scales2, ((0, 256),))
-            elif lo > 128:
-                gather(slot_bytes2, scales2, ((lo, hi),))
-            gather(slot_words[2], codes[2], ((lo, hi),))
+        gather(slot_words[1], codes[1], (third,))
+        for piece in (first, second):
+            gather(slot_bytes2, scales2, (piece,))
+            gather(slot_words[2], codes[2], (piece,))
+        gather(slot_bytes2, scales2, (third,))
+        gather(slot_words[2], codes[2], ((128, 256), (0, 128)))
 
         def multiply(t, s, passes):
             e = expert_of(s)
@@ -156,21 +159,27 @@ def tile_moe_rag_lin_relu2_kernel(tc, xT, w_words, w_scales, b, gate, offs, pos1
             nc.scalar.activation(y_t[t][:, lo:hi], r_t[t][:, lo:hi], ACT.Square)
 
         early = (640, 512)
-        for t in range(NT):
-            for s in early:
+        for s in early:
+            for t in range(NT):
                 multiply(t, s, (0, 1))
 
+        chunks = {3: (640, 768, 896), 2: (512, 384), 1: (256, 128), 0: (0,)}
+        order = [(0, 3), (1, 3), (2, 3)]
+        order += [(0, 2), (0, 1), (0, 0), (3, 3)]
+        for t in range(1, NT):
+            order += [(t, 2), (t, 1), (t, 0)]
+        done = []
         halves = ((0, T // 2), (T // 2, T))
-        for t in range(NT):
-            before = None
-            for e, chunks in ((3, (640, 768, 896)), (2, (512, 384)), (1, (256, 128)), (0, (0,))):
-                for s in chunks:
-                    multiply(t, s, (2,) if s in early else (0, 1, 2))
-                relu(t, e)
-                if before is not None:
-                    square(t, before)
-                before = e
-            square(t, before)
+        for t, e in order:
+            for s in chunks[e]:
+                multiply(t, s, (2,) if s in early else (0, 1, 2))
+            relu(t, e)
+            done.append((t, e))
+            if len(done) > 1 and done[-2][1] != 0:
+                square(*done[-2])
+            if e > 0:
+                continue
+            square(t, e)
             nc.vector.tensor_tensor(one_t[t][:], y_t[t][:].indirect(pos1_t[:]), gate_t[t][:, 0, :], MULT)
             for lo, hi in halves:
                 nc.vector.tensor_tensor(two_t[t][:, lo:hi], y_t[t][:].indirect(pos2_t[:, lo // 16 : hi // 16]), gate_t[t][:, 1, lo:hi], MULT)

@@ -27,6 +27,12 @@ FLOPS = 2 * K * N * SLOTS
 PIECES = ((640, 1024), (256, 640), (0, 256))
 
 
+def next_piece(slot):
+    for i, (lo, hi) in enumerate(PIECES):
+        if lo <= slot < hi:
+            return i, lo
+
+
 def expert_of(slot):
     return max(e for e in range(E) if STARTS[e] <= slot)
 
@@ -35,7 +41,7 @@ def tile_moe_rag_lin_relu2_kernel(tc, xT, w_words, w_scales, b, gate, offs, pos1
     nc = tc.nc
     with ExitStack() as ctx:
         keep = ctx.enter_context(tc.tile_pool(name="keep", bufs=1))
-        psum = ctx.enter_context(tc.psum_pool(name="psum", bufs=1))
+        psum = ctx.enter_context(tc.psum_pool(name="psum", bufs=8))
 
         offs_t = keep.tile([P, SLOTS // 16], U16, name="offs_t")
         pos1_t = keep.tile([P, T // 16], U16, name="pos1_t")
@@ -50,25 +56,25 @@ def tile_moe_rag_lin_relu2_kernel(tc, xT, w_words, w_scales, b, gate, offs, pos1
         slot_bytes0 = keep.tile([P, SLOTS], U8, name="slot_bytes0", align_bytes=64)
         slot_bytes2 = keep.tile([P, SLOTS], U8, name="slot_bytes2", align_bytes=64)
         slot_bytes = [slot_bytes0, slot_bytes01, slot_bytes2]
-        w_t = [keep.tile([P, PASSES, 2 * N], U8, name=f"w{e}", align_bytes=64) for e in range(E)]
+        w_rest = keep.tile([P, 3 * PASSES, 2 * N], U8, name="w_rest", align_bytes=64)
+        w_three = keep.tile([P, PASSES, 2 * N], U8, name="w_three", align_bytes=64)
         ws_t = keep.tile([P, E * PASSES, N], U8, name="ws_t", align_bytes=64)
         b_t = keep.tile([P, NT, E], F32, name="b_t")
-        gate_t = [keep.tile([P, 2, T], F32, name=f"gate{t}") for t in range(NT)]
+        gate_first = keep.tile([P, 2, T], F32, name="gate_first")
+        gate_rest = [keep.tile([P, NT - 1, T], F32, name=f"gate_rest{c}") for c in range(2)]
         r_t = [keep.tile([P, SLOTS], F32, name=f"r{t}") for t in range(NT)]
         y_t = [keep.tile([P, SLOTS], F32, name=f"y{t}") for t in range(NT)]
         one_t = [keep.tile([P, T], F32, name=f"one{t}") for t in range(NT)]
         two_t = [keep.tile([P, T], F32, name=f"two{t}") for t in range(NT)]
         sum_t = [keep.tile([P, T], F32, name=f"sum{t}") for t in range(NT)]
         warm = keep.tile([P, 1], F32, name="warm")
-        bank_a = [psum.tile([P, 512], F32, name=f"bank_a{t}") for t in range(NT)]
-        bank_b = [psum.tile([P, 512], F32, name=f"bank_b{t}") for t in range(NT)]
+        banks = {}
 
         def bank(t, lo, hi):
-            if hi <= 128:
-                return bank_a[t][:, lo:hi]
-            if lo >= 640:
-                return bank_a[t][:, lo - 512 : hi - 512]
-            return bank_b[t][:, lo - 128 : hi - 128]
+            i, start = next_piece(lo)
+            if (t, i) not in banks:
+                banks[t, i] = psum.tile([P, 512], F32, name="bank")
+            return banks[t, i][:, lo - start : hi - start]
 
         def load_x(a, lo, hi):
             nc.sync.dma_start(out=raw[a][:, :, lo:hi], in_=xT[512 * a : 512 * (a + 1), lo:hi].rearrange("(p j) w -> p j w", j=4))
@@ -87,13 +93,17 @@ def tile_moe_rag_lin_relu2_kernel(tc, xT, w_words, w_scales, b, gate, offs, pos1
         by_row = w_scales.rearrange("e a q n -> q (e a) n")
         for q in range(4):
             nc.sync.dma_start(out=ws_t[32 * q : 32 * q + 4, :, :].bitcast(I32), in_=by_row[4 * q : 4 * q + 4, :, :].bitcast(I32))
-        for e in (3, 2, 1, 0):
-            nc.sync.dma_start(out=w_t[e][:], in_=w_words[e].rearrange("a p n -> p a n"))
-        nc.sync.dma_start(out=b_t[:], in_=b.rearrange("(t p) e -> p t e", p=P))
         nc.sync.dma_start(pos1_t[:], pos1)
         nc.sync.dma_start(pos2_t[:], pos2)
-        for t in range(NT):
-            nc.sync.dma_start(out=gate_t[t][:], in_=gate[:, P * t : P * (t + 1), :].rearrange("c p w -> p c w"))
+        nc.sync.dma_start(out=w_three[:], in_=w_words[3].rearrange("a p n -> p a n"))
+        nc.sync.dma_start(out=w_rest[:], in_=w_words[0:3].rearrange("e a p n -> p (e a) n"))
+        nc.sync.dma_start(out=b_t[:], in_=b.rearrange("(t p) e -> p t e", p=P))
+        nc.sync.dma_start(out=gate_first[:], in_=gate[:, 0:P, :].rearrange("c p w -> p c w"))
+        for c in range(2):
+            nc.sync.dma_start(out=gate_rest[c][:], in_=gate[c, P:, :].rearrange("(t p) w -> p t w", p=P))
+
+        def gate_of(c, t, lo, hi):
+            return gate_first[:, c, lo:hi] if t == 0 else gate_rest[c][:, t - 1, lo:hi]
 
         def cast(engine_copy, a, lo, hi):
             engine_copy(
@@ -124,10 +134,8 @@ def tile_moe_rag_lin_relu2_kernel(tc, xT, w_words, w_scales, b, gate, offs, pos1
         gather(slot_words[0], codes[0], (third,))
         quantize(1, scales01, 0, T)
         gather(slot_bytes01, scales01, PIECES)
-        for q in range(4):
-            nc.scalar.dma_start(
-                out=slot_bytes0[32 * q : 32 * q + 4, :].bitcast(I32), in_=slot_bytes01[32 * q + 4 : 32 * q + 8, :].bitcast(I32)
-            )
+        for lo, hi in ((0, 64), (64, 96), (96, 100)):
+            nc.scalar.dma_start(out=slot_bytes0[lo:hi, :].bitcast(I32), in_=slot_bytes01[lo + 4 : hi + 4, :].bitcast(I32))
         gather(slot_words[1], codes[1], (first, second))
         quantize(2, scales2, 0, T)
         gather(slot_words[1], codes[1], (third,))
@@ -139,10 +147,11 @@ def tile_moe_rag_lin_relu2_kernel(tc, xT, w_words, w_scales, b, gate, offs, pos1
 
         def multiply(t, s, passes):
             e = expert_of(s)
+            w_e = w_three if e == 3 else w_rest[:, PASSES * e : PASSES * (e + 1), :]
             for a in passes:
                 nc.tensor.matmul_mx(
                     out=bank(t, s, s + P),
-                    lhsT=w_t[e][:, a, 2 * P * t : 2 * P * (t + 1)].bitcast(FP4X4),
+                    lhsT=w_e[:, a, 2 * P * t : 2 * P * (t + 1)].bitcast(FP4X4),
                     lhsT_scale=ws_t[:, PASSES * e + a, P * t : P * (t + 1)],
                     rhs=slot_words[a][:, s : s + P].bitcast(FP8X4),
                     rhs_scale=slot_bytes[a][:, s : s + P],
@@ -150,39 +159,42 @@ def tile_moe_rag_lin_relu2_kernel(tc, xT, w_words, w_scales, b, gate, offs, pos1
                     stop=(a == PASSES - 1),
                 )
 
-        def relu(t, e):
-            lo, hi = STARTS[e], STARTS[e] + COUNTS[e]
+        def relu(t, lo, hi):
+            e = expert_of(lo)
             nc.scalar.activation(r_t[t][:, lo:hi], bank(t, lo, hi), ACT.Relu, bias=b_t[:, t, e : e + 1])
 
-        def square(t, e):
-            lo, hi = STARTS[e], STARTS[e] + COUNTS[e]
+        def square(t, lo, hi):
             nc.scalar.activation(y_t[t][:, lo:hi], r_t[t][:, lo:hi], ACT.Square)
 
-        early = (640, 512)
-        for s in early:
-            for t in range(NT):
-                multiply(t, s, (0, 1))
+        early = [(0, 640), (1, 640), (0, 512), (1, 512), (2, 640), (2, 512), (0, 128), (1, 128)]
+        for t, s in early:
+            multiply(t, s, (0, 1))
 
-        chunks = {3: (640, 768, 896), 2: (512, 384), 1: (256, 128), 0: (0,)}
-        order = [(0, 3), (1, 3), (2, 3)]
-        order += [(0, 2), (0, 1), (0, 0), (3, 3)]
-        for t in range(1, NT):
-            order += [(t, 2), (t, 1), (t, 0)]
-        done = []
-        halves = ((0, T // 2), (T // 2, T))
-        for t, e in order:
-            for s in chunks[e]:
-                multiply(t, s, (2,) if s in early else (0, 1, 2))
-            relu(t, e)
-            done.append((t, e))
-            if len(done) > 1 and done[-2][1] != 0:
-                square(*done[-2])
-            if e > 0:
+        halves = ((0, 384), (384, T))
+        waiting = []
+
+        def part(t, chunks, relus):
+            for s in chunks:
+                multiply(t, s, (2,) if (t, s) in early else (0, 1, 2))
+            for lo, hi in relus:
+                relu(t, lo, hi)
+                while waiting:
+                    square(*waiting.pop())
+                waiting.append((t, lo, hi))
+
+        top = ((640, 768, 896), ((640, 1024),))
+        middle = ((512, 384, 256), ((384, 640), (256, 384)))
+        bottom = ((128, 0), ((128, 256), (0, 128)))
+        order = ((0, top), (1, top), (0, middle), (0, bottom), (1, middle), (1, bottom))
+        order += ((2, top), (2, middle), (2, bottom), (3, top), (3, middle), (3, bottom))
+        for t, step in order:
+            part(t, *step)
+            if step is not bottom:
                 continue
-            square(t, e)
-            nc.vector.tensor_tensor(one_t[t][:], y_t[t][:].indirect(pos1_t[:]), gate_t[t][:, 0, :], MULT)
+            square(*waiting.pop())
+            nc.vector.tensor_tensor(one_t[t][:], y_t[t][:].indirect(pos1_t[:]), gate_of(0, t, 0, T), MULT)
             for lo, hi in halves:
-                nc.vector.tensor_tensor(two_t[t][:, lo:hi], y_t[t][:].indirect(pos2_t[:, lo // 16 : hi // 16]), gate_t[t][:, 1, lo:hi], MULT)
+                nc.vector.tensor_tensor(two_t[t][:, lo:hi], y_t[t][:].indirect(pos2_t[:, lo // 16 : hi // 16]), gate_of(1, t, lo, hi), MULT)
             for lo, hi in halves:
                 nc.vector.tensor_tensor(sum_t[t][:, lo:hi], one_t[t][:, lo:hi], two_t[t][:, lo:hi], ADD)
                 if t == NT - 1:

from contextlib import ExitStack

import concourse.mybir as mybir

K, T, E, N = 1536, 512, 4, 512
COUNTS = (128, 256, 256, 384)
STARTS = (0, 128, 384, 640)
SLOTS = 1024
P = 128
PASSES = K // 512
NT = N // P

F32 = mybir.dt.float32
BF16 = mybir.dt.bfloat16
U32 = mybir.dt.uint32
I32 = mybir.dt.int32
U16 = mybir.dt.uint16
U8 = mybir.dt.uint8
FP8X4 = mybir.dt.float8_e4m3fn_x4
FP4X4 = mybir.dt.float4_e2m1fn_x4
ACT = mybir.ActivationFunctionType
MULT = mybir.AluOpType.mult
ADD = mybir.AluOpType.add

FLOPS = 2 * K * N * SLOTS

PIECES = ((640, 1024), (256, 640), (0, 256))


def next_piece(slot):
    for i, (lo, hi) in enumerate(PIECES):
        if lo <= slot < hi:
            return i, lo


def expert_of(slot):
    return max(e for e in range(E) if STARTS[e] <= slot)


def tile_moe_rag_lin_relu2_kernel(tc, xT, w_words, w_scales, b, gate, offs, pos1, pos2, out):
    nc = tc.nc
    with ExitStack() as ctx:
        keep = ctx.enter_context(tc.tile_pool(name="keep", bufs=1))
        psum = ctx.enter_context(tc.psum_pool(name="psum", bufs=8))

        offs_t = keep.tile([P, SLOTS // 16], U16, name="offs_t")
        pos1_t = keep.tile([P, T // 16], U16, name="pos1_t")
        pos2_t = keep.tile([P, T // 16], U16, name="pos2_t")
        raw = [keep.tile([P, 4, T], F32, name=f"raw{a}") for a in range(PASSES)]
        grouped = [keep.tile([P, T, 4], BF16, name=f"grouped{a}", align_bytes=64) for a in range(PASSES)]
        codes = [keep.tile([P, T], U32, name=f"codes{a}", align_bytes=64) for a in range(PASSES)]
        scales01 = keep.tile([P, T], U8, name="scales01", align_bytes=64)
        scales2 = keep.tile([P, T], U8, name="scales2", align_bytes=64)
        slot_words = [keep.tile([P, SLOTS], U32, name=f"slot_words{a}", align_bytes=64) for a in range(PASSES)]
        slot_bytes01 = keep.tile([P, SLOTS], U8, name="slot_bytes01", align_bytes=64)
        slot_bytes0 = keep.tile([P, SLOTS], U8, name="slot_bytes0", align_bytes=64)
        slot_bytes2 = keep.tile([P, SLOTS], U8, name="slot_bytes2", align_bytes=64)
        slot_bytes = [slot_bytes0, slot_bytes01, slot_bytes2]
        w_rest = keep.tile([P, 3 * PASSES, 2 * N], U8, name="w_rest", align_bytes=64)
        w_three = keep.tile([P, PASSES, 2 * N], U8, name="w_three", align_bytes=64)
        ws_t = keep.tile([P, E * PASSES, N], U8, name="ws_t", align_bytes=64)
        b_t = keep.tile([P, NT, E], F32, name="b_t")
        gate_first = keep.tile([P, 2, T], F32, name="gate_first")
        gate_rest = [keep.tile([P, NT - 1, T], F32, name=f"gate_rest{c}") for c in range(2)]
        r_t = [keep.tile([P, SLOTS], F32, name=f"r{t}") for t in range(NT)]
        y_t = [keep.tile([P, SLOTS], F32, name=f"y{t}") for t in range(NT)]
        one_t = [keep.tile([P, T], F32, name=f"one{t}") for t in range(NT)]
        two_t = [keep.tile([P, T], F32, name=f"two{t}") for t in range(NT)]
        sum_t = [keep.tile([P, T], F32, name=f"sum{t}") for t in range(NT)]
        warm = keep.tile([P, 1], F32, name="warm")
        banks = {}

        def bank(t, lo, hi):
            i, start = next_piece(lo)
            if (t, i) not in banks:
                banks[t, i] = psum.tile([P, 512], F32, name="bank")
            return banks[t, i][:, lo - start : hi - start]

        def load_x(a, lo, hi):
            nc.sync.dma_start(out=raw[a][:, :, lo:hi], in_=xT[512 * a : 512 * (a + 1), lo:hi].rearrange("(p j) w -> p j w", j=4))

        load_x(0, 0, 256)
        load_x(0, 256, T)
        nc.sync.dma_start(offs_t[:], offs)
        load_x(1, 0, T)
        load_x(2, 0, T)
        nc.vector.memset(ws_t[:].rearrange("p a n -> p (a n)").bitcast(I32), 0)
        nc.gpsimd.memset(scales01[:], 0)
        nc.gpsimd.memset(scales2[:], 0)
        nc.gpsimd.memset(slot_bytes0[:], 0)
        nc.vector.memset(warm[:], 0.0)
        nc.scalar.activation(warm[:], warm[:], ACT.Relu)
        by_row = w_scales.rearrange("e a q n -> q (e a) n")
        for q in range(4):
            nc.sync.dma_start(out=ws_t[32 * q : 32 * q + 4, :, :].bitcast(I32), in_=by_row[4 * q : 4 * q + 4, :, :].bitcast(I32))
        nc.sync.dma_start(pos1_t[:], pos1)
        nc.sync.dma_start(pos2_t[:], pos2)
        nc.sync.dma_start(out=w_three[:], in_=w_words[3].rearrange("a p n -> p a n"))
        nc.sync.dma_start(out=w_rest[:], in_=w_words[0:3].rearrange("e a p n -> p (e a) n"))
        nc.sync.dma_start(out=b_t[:], in_=b.rearrange("(t p) e -> p t e", p=P))
        nc.sync.dma_start(out=gate_first[:], in_=gate[:, 0:P, :].rearrange("c p w -> p c w"))
        for c in range(2):
            nc.sync.dma_start(out=gate_rest[c][:], in_=gate[c, P:, :].rearrange("(t p) w -> p t w", p=P))

        def gate_of(c, t, lo, hi):
            return gate_first[:, c, lo:hi] if t == 0 else gate_rest[c][:, t - 1, lo:hi]

        def cast(engine_copy, a, lo, hi):
            engine_copy(
                out=grouped[a][:, lo:hi, :].rearrange("p (c i) j -> p c j i", i=4),
                in_=raw[a][:, :, lo:hi].rearrange("p j (c i) -> p c j i", i=4),
            )

        def quantize(a, plane, lo, hi):
            nc.vector.quantize_mx(
                out=codes[a][:, lo:hi].bitcast(FP8X4), scales=plane[:, lo:hi], in_=grouped[a][:, lo:hi, :].rearrange("p w j -> p (w j)")
            )

        def gather(out, table, pieces):
            for lo, hi in pieces:
                nc.vector.tensor_copy(out[:, lo:hi], table[:].indirect(offs_t[:, lo // 16 : hi // 16]))

        cast(nc.vector.tensor_copy, 0, 0, 256)
        quantize(0, scales01[4:P, :], 0, 256)
        cast(nc.vector.tensor_copy, 0, 256, 416)
        cast(nc.scalar.copy, 0, 416, T)
        quantize(0, scales01[4:P, :], 256, T)
        cast(nc.scalar.copy, 1, 192, T)
        cast(nc.scalar.copy, 2, 0, T // 2)
        cast(nc.scalar.copy, 2, T // 2, T)
        first, second, third = PIECES
        gather(slot_words[0], codes[0], (first, second))
        cast(nc.vector.tensor_copy, 1, 0, 192)
        gather(slot_words[0], codes[0], (third,))
        quantize(1, scales01, 0, T)
        gather(slot_bytes01, scales01, PIECES)
        for lo, hi in ((0, 64), (64, 96), (96, 100)):
            nc.scalar.dma_start(out=slot_bytes0[lo:hi, :].bitcast(I32), in_=slot_bytes01[lo + 4 : hi + 4, :].bitcast(I32))
        gather(slot_words[1], codes[1], (first, second))
        quantize(2, scales2, 0, T)
        gather(slot_words[1], codes[1], (third,))
        for piece in (first, second):
            gather(slot_bytes2, scales2, (piece,))
            gather(slot_words[2], codes[2], (piece,))
        gather(slot_bytes2, scales2, (third,))
        gather(slot_words[2], codes[2], ((128, 256), (0, 128)))

        def multiply(t, s, passes):
            e = expert_of(s)
            w_e = w_three if e == 3 else w_rest[:, PASSES * e : PASSES * (e + 1), :]
            for a in passes:
                nc.tensor.matmul_mx(
                    out=bank(t, s, s + P),
                    lhsT=w_e[:, a, 2 * P * t : 2 * P * (t + 1)].bitcast(FP4X4),
                    lhsT_scale=ws_t[:, PASSES * e + a, P * t : P * (t + 1)],
                    rhs=slot_words[a][:, s : s + P].bitcast(FP8X4),
                    rhs_scale=slot_bytes[a][:, s : s + P],
                    start=(a == 0),
                    stop=(a == PASSES - 1),
                )

        def relu(t, lo, hi):
            e = expert_of(lo)
            nc.scalar.activation(r_t[t][:, lo:hi], bank(t, lo, hi), ACT.Relu, bias=b_t[:, t, e : e + 1])

        def square(t, lo, hi):
            nc.scalar.activation(y_t[t][:, lo:hi], r_t[t][:, lo:hi], ACT.Square)

        early = [(0, 640), (1, 640), (0, 512), (1, 512), (2, 640), (2, 512), (0, 128), (1, 128)]
        for t, s in early:
            multiply(t, s, (0, 1))

        halves = ((0, 384), (384, T))
        waiting = []

        def part(t, chunks, relus):
            for s in chunks:
                multiply(t, s, (2,) if (t, s) in early else (0, 1, 2))
            for lo, hi in relus:
                relu(t, lo, hi)
                while waiting:
                    square(*waiting.pop())
                waiting.append((t, lo, hi))

        top = ((640, 768, 896), ((640, 1024),))
        middle = ((512, 384, 256), ((384, 640), (256, 384)))
        bottom = ((128, 0), ((128, 256), (0, 128)))
        order = ((0, top), (1, top), (0, middle), (0, bottom), (1, middle), (1, bottom))
        order += ((2, top), (2, middle), (2, bottom), (3, top), (3, middle), (3, bottom))
        for t, step in order:
            part(t, *step)
            if step is not bottom:
                continue
            square(*waiting.pop())
            nc.vector.tensor_tensor(one_t[t][:], y_t[t][:].indirect(pos1_t[:]), gate_of(0, t, 0, T), MULT)
            for lo, hi in halves:
                nc.vector.tensor_tensor(two_t[t][:, lo:hi], y_t[t][:].indirect(pos2_t[:, lo // 16 : hi // 16]), gate_of(1, t, lo, hi), MULT)
            for lo, hi in halves:
                nc.vector.tensor_tensor(sum_t[t][:, lo:hi], one_t[t][:, lo:hi], two_t[t][:, lo:hi], ADD)
                if t == NT - 1:
                    (nc.sync if lo == 0 else nc.scalar).dma_start(out=out[P * t : P * (t + 1), lo:hi], in_=sum_t[t][:, lo:hi])
            if t < NT - 1:
                nc.sync.dma_start(out=out[P * t : P * (t + 1), :], in_=sum_t[t][:])
